import numpy as np, ml_dtypes
CORES = [2,3,6,7,58,59,62,63,114,115,118,119]
N = 12
S, B = 2, 256
def setup_inputs(rng):
    return {"x": rng.standard_normal((N, 128, S * B), dtype=np.float32).astype(ml_dtypes.bfloat16), "gate": (0.9375 + 0.03125 * rng.standard_normal((N, 128, S * B), dtype=np.float32)).astype(ml_dtypes.bfloat16)}
def setup_inputs_big(rng):
    d = setup_inputs(rng)
    for k in ("x",): d[k] = (d[k].astype(np.float32) * 1048576.0).astype(d[k].dtype)
    return d
def setup_inputs_small(rng):
    d = setup_inputs(rng)
    for k in ("x",): d[k] = (d[k].astype(np.float32) * (1 / 1048576.0)).astype(d[k].dtype)
    return d
def setup_inputs_apart(rng):
    d = setup_inputs(rng)
    f = (10.0 ** rng.permutation(np.linspace(-1.5, 1.5, N))).astype(np.float32).reshape(N, 1, 1)
    for k in ("x",): d[k] = (d[k].astype(np.float32) * f).astype(d[k].dtype)
    return d
def reference(x, gate):
    X, GATE = x.astype(np.float64), gate.astype(np.float64)
    y = np.zeros((N, 128, S * B)); h = np.zeros((128, B))
    for r in range(N):
        for s in range(S):
            h = GATE[r][:, B * s:B * s + B] * h + X[r][:, B * s:B * s + B]
            y[r][:, B * s:B * s + B] = h
    return {"y": y.astype(ml_dtypes.bfloat16)}

@@ -1,0 +1,222 @@
+from concourse.bass import DstId, RemoteDMATransfer
+from concourse.mybir import AluOpType
+
+W = 256
+BF = "bfloat16"
+SCRATCH = {
+    "G": ("sbuf", [128, 2 * W], BF),
+    "X": ("sbuf", [128, 2 * W], BF),
+    "Ab": ("sbuf", [128, 4 * W], BF),
+    "Bb": ("sbuf", [128, 4 * W], BF),
+    "Tb": ("sbuf", [128, W], BF),
+    "U": ("sbuf", [128, 3 * W], BF),
+    "AT": ("sbuf", [128, W], BF),
+    "Am": ("sbuf", [128, W], BF),
+    "Bm": ("sbuf", [128, W], BF),
+    "Bz": ("sbuf", [128, W], BF),
+    "Pr": ("sbuf", [128, W], BF),
+    "Be": ("sbuf", [128, W], BF),
+    "Be2": ("sbuf", [128, W], BF),
+    "Y": ("sbuf", [128, 2 * W], BF),
+    "Pg": ("psum", [128, 2 * W], "float32"),
+    "Ps": ("psum", [128, 2 * W], "float32"),
+    "Pt": ("psum", [128, 2 * W], "float32"),
+    "Pw": ("psum", [128, 2 * W], "float32"),
+    "Pa": ("psum", [128, 2 * W], "float32"),
+    "Pc": ("psum", [128, 2 * W], "float32"),
+    "Pm": ("psum", [128, 2 * W], "float32"),
+}
+SEMAPHORES = ["ldg", "ldx", "v", "sA", "sT", "sB", "sAT", "sU", "sY0", "sY1", "arrA", "arrB", "arrAm", "arrBm",
+              "arrBz", "loc", "st"]
+
+
+def _bits(mask):
+    return [b for b in range(32) if (mask >> b) & 1]
+
+
+def rank_program(g, core, T, topo):
+    if T.rank_of(core) is None:
+        return
+    groups = []
+    for c in T.cores:
+        if groups and topo.chip(groups[-1][0]) == topo.chip(c):
+            groups[-1].append(c)
+        else:
+            groups.append([c])
+    assert len(groups) == 3 and all(len(q) == 4 for q in groups)
+    k = [core in q for q in groups].index(True)
+    grp = groups[k]
+    i = grp.index(core)
+    n, last = 4, 2
+
+    def sl(buf, j, m=1):
+        return buf[:, j * W:(j + m) * W]
+
+    def engines(src, dsts):
+        m = topo.mask(src, dsts[0])
+        for d in dsts[1:]:
+            m &= topo.mask(src, d)
+        return m
+
+    def partner(a, b, c):
+        sa = sorted(groups[a], key=lambda q: (topo.die(q), q))
+        sb = sorted(groups[b], key=lambda q: (topo.die(q), q))
+        return sb[sa.index(c)]
+
+    def hop1_dests(kk, j):
+        return [c for jj, c in enumerate(groups[kk]) if (jj != j if kk < last else jj > j)]
+
+    def sends_a(kk, j):
+        return bool(hop1_dests(kk, j)) and not (kk == 0 and j == 0)
+
+    def hop2_dests(kk, c):
+        return [partner(kk, b, c) for b in range(kk + 1, last + 1)]
+
+    cnt = {}
+    waited = {}
+
+    def bump(name, m):
+        cnt[name] = cnt.get(name, 0) + m
+
+    def wait(q, qn, name):
+        if cnt.get(name, 0) > waited.get((qn, name), 0):
+            q.wait_ge(T.sem[name], cnt[name])
+            waited[(qn, name)] = cnt[name]
+
+    for j, c in enumerate(grp):
+        if c != core and core in hop1_dests(k, j):
+            e = len(_bits(engines(c, hop1_dests(k, j))))
+            bump("arrB", e)
+            if sends_a(k, j):
+                bump("arrA", e)
+    for kk in range(k):
+        for c in groups[kk]:
+            if core in hop2_dests(kk, c):
+                e = len(_bits(engines(c, hop2_dests(kk, c))))
+                if kk == 0:
+                    bump("arrBz", e)
+                else:
+                    bump("arrAm", e)
+                    bump("arrBm", e)
+
+    vsigs = ["v", "sA", "sT", "sB", "sAT", "sU", "sY0", "sY1"]
+
+    def vop(out, a, b=None, op=None, sig="v", deps=()):
+        for d in deps:
+            wait(g.vector, "V", d)
+        for s in vsigs:
+            wait(g.vector, "V", s)
+        if b is None:
+            ins = g.vector.tensor_copy(out, a)
+        else:
+            ins = g.vector.tensor_tensor(out, a, b, op)
+        ins.then_inc(T.sem[sig], 1)
+        bump(sig, 1)
+
+    MUL, ADD = AluOpType.mult, AluOpType.add
+
+    def send(srcs, dst_ap, dests, sem, deps):
+        for d in deps:
+            wait(g, "G", d)
+        for d in dests:
+            assert topo.may_write(core, d)
+        m = engines(core, dests)
+        ids = [DstId(rid=topo.addr(d)[0], pnc=topo.addr(d)[1]) for d in dests]
+        tr = RemoteDMATransfer(dst_ids=ids, dma_engine_mask=m, remote_sem=T.sem[sem], srcs=list(srcs),
+                               dsts=[dst_ap for _ in dests], alu_op=(1 if len(srcs) > 1 else 0))
+        g.remote_dma_fused([tr], local_sem=T.sem.loc)
+        bump("loc", len(_bits(m)))
+
+    G0, G1, X0, X1 = sl(T.G, 0), sl(T.G, 1), sl(T.X, 0), sl(T.X, 1)
+    g0p, g1p = sl(T.Pg, 0), sl(T.Pg, 1)
+    Y0, Y1 = sl(T.Y, 0), sl(T.Y, 1)
+
+    g.sync.dma_start(T.G[:], T.gate[:]).then_inc(T.sem.ldg, 16)
+    bump("ldg", 16)
+    g.scalar.dma_start(T.X[:], T.x[:]).then_inc(T.sem.ldx, 16)
+    bump("ldx", 16)
+
+    d1 = hop1_dests(k, i)
+    vop(g1p, G1, deps=["ldg"])
+    if sends_a(k, i):
+        vop(sl(T.Ab, i), G0, g1p, MUL, sig="sA")
+        send([sl(T.Ab, i)], sl(T.Ab, i), d1, "arrA", ["sA"])
+    if d1:
+        vop(T.Tb[:], X0, g1p, MUL, sig="sT", deps=["ldx"])
+        send([T.Tb[:], X1], sl(T.Bb, i), d1, "arrB", ["sT", "ldx"])
+    if k < last:
+        vop(sl(T.Bb, i), T.Tb[:], X1, ADD, sig="sB")
+    if k > 0 or i > 0:
+        vop(g0p, G0)
+
+    if k < last:
+        d2 = hop2_dests(k, core)
+        S0, S1, S2 = sl(T.Ps, 0), sl(T.Ps, 1), sl(T.Pt, 0)
+        vop(S2, sl(T.Ab, 3), deps=["arrA"])
+        vop(S1, sl(T.Ab, 2), S2, MUL)
+        vop(S0, sl(T.Ab, 1), S1, MUL)
+        if k > 0:
+            vop(T.AT[:], sl(T.Ab, 0), S0, MUL, sig="sAT")
+            send([T.AT[:]], T.Am[:], d2, "arrAm", ["sAT"])
+        vop(sl(T.U, 0, 2), sl(T.Bb, 0, 2), T.Ps[:], MUL, sig="sU", deps=["arrB"])
+        vop(sl(T.U, 2), sl(T.Bb, 2), S2, MUL, sig="sU")
+        send([sl(T.U, 0), sl(T.U, 1), sl(T.U, 2), sl(T.Bb, 3)], (T.Bz[:] if k == 0 else T.Bm[:]), d2,
+             ("arrBz" if k == 0 else "arrBm"), ["sU", "sB", "arrB"])
+
+    alpha, beta = g0p, X0
+    if i > 0:
+        w = {i - 1: g0p}
+        r = g0p
+        for j in range(i - 1, (0 if k > 0 else 1) - 1, -1):
+            out = sl(T.Pw, j - 1) if j > 0 else sl(T.Pa, 0)
+            vop(out, sl(T.Ab, j), r, MUL, deps=["arrA"])
+            r = out
+            if j > 0:
+                w[j - 1] = out
+        alpha = r
+        fin = Y0 if k == 0 else T.Be[:]
+        fsig = "sY0" if k == 0 else "v"
+        acc = [sl(T.Pc, 0), sl(T.Pc, 1)]
+        vop(acc[0], sl(T.Bb, i - 1), g0p, MUL, deps=["arrB"])
+        cur = 0
+        if i == 1:
+            vop(fin, X0, acc[0], ADD, sig=fsig, deps=["ldx"])
+        else:
+            vop(acc[1], X0, acc[0], ADD, deps=["ldx"])
+            cur = 1
+        for j in range(i - 2, -1, -1):
+            vop(T.Pr[:], sl(T.Bb, j), w[j], MUL)
+            if j == 0:
+                vop(fin, T.Pr[:], acc[cur], ADD, sig=fsig)
+            else:
+                vop(acc[1 - cur], T.Pr[:], acc[cur], ADD)
+                cur = 1 - cur
+        beta = fin
+
+    pm, pq = sl(T.Pm, 0), sl(T.Pm, 1)
+    y0_src, y1_src, y0_dep, y1_dep = Y0, Y1, "sY0", "sY1"
+    if k == 0:
+        if i == 0:
+            y0_src, y0_dep, y1_src, y1_dep = X0, "ldx", sl(T.Bb, 0), "sB"
+    elif k == 1:
+        vop(pm, T.Bz[:], alpha, MUL, deps=["arrBz"])
+        vop(Y0, beta, pm, ADD, sig="sY0", deps=["ldx"])
+    else:
+        a0 = sl(T.Pt, 1)
+        vop(a0, T.Am[:], alpha, MUL, deps=["arrAm"])
+        vop(pm, T.Bm[:], alpha, MUL, deps=["arrBm"])
+        vop(T.Be2[:], beta, pm, ADD, deps=["ldx"])
+        vop(pq, T.Bz[:], a0, MUL, deps=["arrBz"])
+        vop(Y0, T.Be2[:], pq, ADD, sig="sY0")
+    if not (k == 0 and i == 0):
+        vop(pm, Y0, g1p, MUL)
+        vop(Y1, X1, pm, ADD, sig="sY1", deps=["ldx"])
+
+    wait(g.scalar, "C", y0_dep)
+    g.scalar.dma_start(T.y[:, 0:W], y0_src).then_inc(T.sem.st, 16)
+    wait(g.sync, "S", y1_dep)
+    g.sync.dma_start(T.y[:, W:2 * W], y1_src).then_inc(T.sem.st, 16)
+    bump("st", 32)
+
+    for name in SEMAPHORES:
+        wait(g, "G", name)

@@ -6,28 +6,24 @@ BF = "bfloat16"
 SCRATCH = {
     "G": ("sbuf", [128, 2 * W], BF),
     "X": ("sbuf", [128, 2 * W], BF),
-    "Ab": ("sbuf", [128, 4 * W], BF),
-    "Bb": ("sbuf", [128, 4 * W], BF),
-    "Tb": ("sbuf", [128, W], BF),
-    "U": ("sbuf", [128, 3 * W], BF),
+    "AB": ("sbuf", [128, 8 * W], BF),
     "AT": ("sbuf", [128, W], BF),
+    "BT": ("sbuf", [128, W], BF),
     "Am": ("sbuf", [128, W], BF),
     "Bm": ("sbuf", [128, W], BF),
     "Bz": ("sbuf", [128, W], BF),
-    "Pr": ("sbuf", [128, W], BF),
     "Be": ("sbuf", [128, W], BF),
     "Be2": ("sbuf", [128, W], BF),
     "Y": ("sbuf", [128, 2 * W], BF),
     "Pg": ("psum", [128, 2 * W], "float32"),
-    "Ps": ("psum", [128, 2 * W], "float32"),
     "Pt": ("psum", [128, 2 * W], "float32"),
-    "Pw": ("psum", [128, 2 * W], "float32"),
+    "Ph": ("psum", [128, 2 * W], "float32"),
+    "Pq": ("psum", [128, 2 * W], "float32"),
     "Pa": ("psum", [128, 2 * W], "float32"),
-    "Pc": ("psum", [128, 2 * W], "float32"),
+    "Pl": ("psum", [128, 2 * W], "float32"),
     "Pm": ("psum", [128, 2 * W], "float32"),
 }
-SEMAPHORES = ["ldg", "ldx", "v", "sA", "sT", "sB", "sAT", "sU", "sY0", "sY1", "arrA", "arrB", "arrAm", "arrBm",
-              "arrBz", "loc", "st"]
+SEMAPHORES = ["ldg", "ldx", "v", "sAB", "sAT", "sBT", "sY0", "sY1", "arr1", "arrAm", "arrBm", "arrBz", "loc", "st"]
 
 
 def _bits(mask):
@@ -52,6 +48,12 @@ def rank_program(g, core, T, topo):
     def sl(buf, j, m=1):
         return buf[:, j * W:(j + m) * W]
 
+    def A(j):
+        return sl(T.AB, 2 * j)
+
+    def B(j):
+        return sl(T.AB, 2 * j + 1)
+
     def engines(src, dsts):
         m = topo.mask(src, dsts[0])
         for d in dsts[1:]:
@@ -65,9 +67,6 @@ def rank_program(g, core, T, topo):
 
     def hop1_dests(kk, j):
         return [c for jj, c in enumerate(groups[kk]) if (jj != j if kk < last else jj > j)]
-
-    def sends_a(kk, j):
-        return bool(hop1_dests(kk, j)) and not (kk == 0 and j == 0)
 
     def hop2_dests(kk, c):
         return [partner(kk, b, c) for b in range(kk + 1, last + 1)]
@@ -85,10 +84,7 @@ def rank_program(g, core, T, topo):
 
     for j, c in enumerate(grp):
         if c != core and core in hop1_dests(k, j):
-            e = len(_bits(engines(c, hop1_dests(k, j))))
-            bump("arrB", e)
-            if sends_a(k, j):
-                bump("arrA", e)
+            bump("arr1", len(_bits(engines(c, hop1_dests(k, j)))))
     for kk in range(k):
         for c in groups[kk]:
             if core in hop2_dests(kk, c):
@@ -99,7 +95,7 @@ def rank_program(g, core, T, topo):
                     bump("arrAm", e)
                     bump("arrBm", e)
 
-    vsigs = ["v", "sA", "sT", "sB", "sAT", "sU", "sY0", "sY1"]
+    vsigs = ["v", "sAB", "sAT", "sBT", "sY0", "sY1"]
 
     def vop(out, a, b=None, op=None, sig="v", deps=()):
         for d in deps:
@@ -115,21 +111,22 @@ def rank_program(g, core, T, topo):
 
     MUL, ADD = AluOpType.mult, AluOpType.add
 
-    def send(srcs, dst_ap, dests, sem, deps):
+    def send(src, dst_ap, dests, sem, deps):
         for d in deps:
             wait(g, "G", d)
         for d in dests:
             assert topo.may_write(core, d)
         m = engines(core, dests)
         ids = [DstId(rid=topo.addr(d)[0], pnc=topo.addr(d)[1]) for d in dests]
-        tr = RemoteDMATransfer(dst_ids=ids, dma_engine_mask=m, remote_sem=T.sem[sem], srcs=list(srcs),
-                               dsts=[dst_ap for _ in dests], alu_op=(1 if len(srcs) > 1 else 0))
+        tr = RemoteDMATransfer(dst_ids=ids, dma_engine_mask=m, remote_sem=T.sem[sem], srcs=[src],
+                               dsts=[dst_ap for _ in dests], alu_op=0)
         g.remote_dma_fused([tr], local_sem=T.sem.loc)
         bump("loc", len(_bits(m)))
 
     G0, G1, X0, X1 = sl(T.G, 0), sl(T.G, 1), sl(T.X, 0), sl(T.X, 1)
     g0p, g1p = sl(T.Pg, 0), sl(T.Pg, 1)
     Y0, Y1 = sl(T.Y, 0), sl(T.Y, 1)
+    first = (k == 0 and i == 0)
 
     g.sync.dma_start(T.G[:], T.gate[:]).then_inc(T.sem.ldg, 16)
     bump("ldg", 16)
@@ -138,77 +135,82 @@ def rank_program(g, core, T, topo):
 
     d1 = hop1_dests(k, i)
     vop(g1p, G1, deps=["ldg"])
-    if sends_a(k, i):
-        vop(sl(T.Ab, i), G0, g1p, MUL, sig="sA")
-        send([sl(T.Ab, i)], sl(T.Ab, i), d1, "arrA", ["sA"])
     if d1:
-        vop(T.Tb[:], X0, g1p, MUL, sig="sT", deps=["ldx"])
-        send([T.Tb[:], X1], sl(T.Bb, i), d1, "arrB", ["sT", "ldx"])
-    if k < last:
-        vop(sl(T.Bb, i), T.Tb[:], X1, ADD, sig="sB")
-    if k > 0 or i > 0:
-        vop(g0p, G0)
+        if not first:
+            vop(A(i), G0, g1p, MUL, sig="sAB")
+        vop(sl(T.Pt, 0), X0, g1p, MUL, deps=["ldx"])
+        vop(B(i), X1, sl(T.Pt, 0), ADD, sig="sAB")
+        piece = B(i) if first else sl(T.AB, 2 * i, 2)
+        send(piece, piece, d1, "arr1", ["sAB"])
 
+    if i <= 1 and not first:
+        vop(g0p, G0)
+    opA = {0: A(0), 1: A(1)}
+    opB = {0: B(0), 1: A(1)}
     if k < last:
-        d2 = hop2_dests(k, core)
-        S0, S1, S2 = sl(T.Ps, 0), sl(T.Ps, 1), sl(T.Pt, 0)
-        vop(S2, sl(T.Ab, 3), deps=["arrA"])
-        vop(S1, sl(T.Ab, 2), S2, MUL)
-        vop(S0, sl(T.Ab, 1), S1, MUL)
-        if k > 0:
-            vop(T.AT[:], sl(T.Ab, 0), S0, MUL, sig="sAT")
-            send([T.AT[:]], T.Am[:], d2, "arrAm", ["sAT"])
-        vop(sl(T.U, 0, 2), sl(T.Bb, 0, 2), T.Ps[:], MUL, sig="sU", deps=["arrB"])
-        vop(sl(T.U, 2), sl(T.Bb, 2), S2, MUL, sig="sU")
-        send([sl(T.U, 0), sl(T.U, 1), sl(T.U, 2), sl(T.Bb, 3)], (T.Bz[:] if k == 0 else T.Bm[:]), d2,
-             ("arrBz" if k == 0 else "arrBm"), ["sU", "sB", "arrB"])
+        if i == 0:
+            vop(sl(T.Ph, 1), B(0))
+            opB[0] = sl(T.Ph, 1)
+            if k > 0:
+                vop(sl(T.Pt, 1), A(0))
+                opA[0] = sl(T.Pt, 1)
+        elif i == 1:
+            vop(sl(T.Pt, 1), A(1))
+            opA[1] = opB[1] = sl(T.Pt, 1)
+
+    top = n if k < last else i
+    PA, PB = {1: A(0)}, {1: B(0)}
+    if k > 0:
+        for j in range(1, top):
+            tot = (j == n - 1)
+            out = T.AT[:] if tot else sl(T.Pa, j - 1)
+            a, b = (opA[0], opA[1]) if j == 1 else (A(j), PA[j])
+            vop(out, a, b, MUL, sig=("sAT" if tot else "v"), deps=["arr1"])
+            PA[j + 1] = out
+        if k < last:
+            send(T.AT[:], T.Am[:], hop2_dests(k, core), "arrAm", ["sAT"])
+    h = sl(T.Ph, 0)
+    for j in range(1, top):
+        tot = (j == n - 1)
+        out = T.BT[:] if tot else sl(T.Pq, j - 1)
+        a, b = (opB[0], opB[1]) if j == 1 else (A(j), PB[j])
+        vop(h, a, b, MUL, deps=["arr1"])
+        vop(out, B(j), h, ADD, sig=("sBT" if tot else "v"))
+        PB[j + 1] = out
+    if k < last:
+        send(T.BT[:], (T.Bz[:] if k == 0 else T.Bm[:]), hop2_dests(k, core), ("arrBz" if k == 0 else "arrBm"), ["sBT"])
 
     alpha, beta = g0p, X0
     if i > 0:
-        w = {i - 1: g0p}
-        r = g0p
-        for j in range(i - 1, (0 if k > 0 else 1) - 1, -1):
-            out = sl(T.Pw, j - 1) if j > 0 else sl(T.Pa, 0)
-            vop(out, sl(T.Ab, j), r, MUL, deps=["arrA"])
-            r = out
-            if j > 0:
-                w[j - 1] = out
-        alpha = r
-        fin = Y0 if k == 0 else T.Be[:]
-        fsig = "sY0" if k == 0 else "v"
-        acc = [sl(T.Pc, 0), sl(T.Pc, 1)]
-        vop(acc[0], sl(T.Bb, i - 1), g0p, MUL, deps=["arrB"])
-        cur = 0
-        if i == 1:
-            vop(fin, X0, acc[0], ADD, sig=fsig, deps=["ldx"])
-        else:
-            vop(acc[1], X0, acc[0], ADD, deps=["ldx"])
-            cur = 1
-        for j in range(i - 2, -1, -1):
-            vop(T.Pr[:], sl(T.Bb, j), w[j], MUL)
-            if j == 0:
-                vop(fin, T.Pr[:], acc[cur], ADD, sig=fsig)
+        if k > 0:
+            alpha = sl(T.Pl, 0)
+            if i == 1:
+                vop(alpha, PA[1], g0p, MUL, deps=["arr1"])
             else:
-                vop(acc[1 - cur], T.Pr[:], acc[cur], ADD)
-                cur = 1 - cur
-        beta = fin
+                vop(alpha, G0, PA[i], MUL)
+        if i == 1:
+            vop(h, PB[1], g0p, MUL, deps=["arr1"])
+        else:
+            vop(h, G0, PB[i], MUL)
+        beta = Y0 if k == 0 else T.Be[:]
+        vop(beta, X0, h, ADD, sig=("sY0" if k == 0 else "v"), deps=["ldx"])
 
     pm, pq = sl(T.Pm, 0), sl(T.Pm, 1)
     y0_src, y1_src, y0_dep, y1_dep = Y0, Y1, "sY0", "sY1"
     if k == 0:
         if i == 0:
-            y0_src, y0_dep, y1_src, y1_dep = X0, "ldx", sl(T.Bb, 0), "sB"
+            y0_src, y0_dep, y1_src, y1_dep = X0, "ldx", B(0), "sAB"
     elif k == 1:
         vop(pm, T.Bz[:], alpha, MUL, deps=["arrBz"])
         vop(Y0, beta, pm, ADD, sig="sY0", deps=["ldx"])
     else:
-        a0 = sl(T.Pt, 1)
+        a0 = sl(T.Pl, 1)
         vop(a0, T.Am[:], alpha, MUL, deps=["arrAm"])
         vop(pm, T.Bm[:], alpha, MUL, deps=["arrBm"])
         vop(T.Be2[:], beta, pm, ADD, deps=["ldx"])
         vop(pq, T.Bz[:], a0, MUL, deps=["arrBz"])
         vop(Y0, T.Be2[:], pq, ADD, sig="sY0")
-    if not (k == 0 and i == 0):
+    if not first:
         vop(pm, Y0, g1p, MUL)
         vop(Y1, X1, pm, ADD, sig="sY1", deps=["ldx"])
 

@@ -1,29 +1,34 @@
 from concourse.bass import DstId, RemoteDMATransfer
-from concourse.mybir import AluOpType
+from concourse.mybir import AluOpType, ActivationFunctionType
 
 W = 256
 BF = "bfloat16"
+NC = 30
 SCRATCH = {
     "G": ("sbuf", [128, 2 * W], BF),
     "X": ("sbuf", [128, 2 * W], BF),
-    "AB": ("sbuf", [128, 8 * W], BF),
+    "Ab": ("sbuf", [128, 4 * W], BF),
+    "Bb": ("sbuf", [128, 4 * W], BF),
+    "Tb": ("sbuf", [128, W], BF),
+    "U": ("sbuf", [128, 3 * W], BF),
     "AT": ("sbuf", [128, W], BF),
-    "BT": ("sbuf", [128, W], BF),
     "Am": ("sbuf", [128, W], BF),
     "Bm": ("sbuf", [128, W], BF),
     "Bz": ("sbuf", [128, W], BF),
-    "Be": ("sbuf", [128, W], BF),
-    "Be2": ("sbuf", [128, W], BF),
+    "Pr": ("sbuf", [128, 2 * W], BF),
+    "Be": ("sbuf", [128, 2 * W], BF),
+    "Be2": ("sbuf", [128, 2 * W], BF),
     "Y": ("sbuf", [128, 2 * W], BF),
     "Pg": ("psum", [128, 2 * W], "float32"),
+    "Ps": ("psum", [128, 2 * W], "float32"),
     "Pt": ("psum", [128, 2 * W], "float32"),
-    "Ph": ("psum", [128, 2 * W], "float32"),
-    "Pq": ("psum", [128, 2 * W], "float32"),
+    "Pw": ("psum", [128, 2 * W], "float32"),
     "Pa": ("psum", [128, 2 * W], "float32"),
-    "Pl": ("psum", [128, 2 * W], "float32"),
+    "Pc": ("psum", [128, 2 * W], "float32"),
     "Pm": ("psum", [128, 2 * W], "float32"),
+    "Pn": ("psum", [128, 2 * W], "float32"),
 }
-SEMAPHORES = ["ldg", "ldx", "v", "sAB", "sAT", "sBT", "sY0", "sY1", "arr1", "arrAm", "arrBm", "arrBz", "loc", "st"]
+SEMAPHORES = ["ldg", "ldx", "arrA", "arrB", "arrAm", "arrBm", "arrBz"] + ["c%d" % q for q in range(NC)] + ["loc", "st"]
 
 
 def _bits(mask):
@@ -48,12 +53,6 @@ def rank_program(g, core, T, topo):
     def sl(buf, j, m=1):
         return buf[:, j * W:(j + m) * W]
 
-    def A(j):
-        return sl(T.AB, 2 * j)
-
-    def B(j):
-        return sl(T.AB, 2 * j + 1)
-
     def engines(src, dsts):
         m = topo.mask(src, dsts[0])
         for d in dsts[1:]:
@@ -67,6 +66,9 @@ def rank_program(g, core, T, topo):
 
     def hop1_dests(kk, j):
         return [c for jj, c in enumerate(groups[kk]) if (jj != j if kk < last else jj > j)]
+
+    def sends_a(kk, j):
+        return bool(hop1_dests(kk, j)) and not (kk == 0 and j == 0)
 
     def hop2_dests(kk, c):
         return [partner(kk, b, c) for b in range(kk + 1, last + 1)]
@@ -84,7 +86,10 @@ def rank_program(g, core, T, topo):
 
     for j, c in enumerate(grp):
         if c != core and core in hop1_dests(k, j):
-            bump("arr1", len(_bits(engines(c, hop1_dests(k, j)))))
+            e = len(_bits(engines(c, hop1_dests(k, j))))
+            bump("arrB", e)
+            if sends_a(k, j):
+                bump("arrA", e)
     for kk in range(k):
         for c in groups[kk]:
             if core in hop2_dests(kk, c):
@@ -95,31 +100,51 @@ def rank_program(g, core, T, topo):
                     bump("arrAm", e)
                     bump("arrBm", e)
 
-    vsigs = ["v", "sAB", "sAT", "sBT", "sY0", "sY1"]
+    MUL, ADD = AluOpType.mult, AluOpType.add
+    used = [0]
 
-    def vop(out, a, b=None, op=None, sig="v", deps=()):
+    def fresh():
+        s = "c%d" % used[0]
+        used[0] += 1
+        bump(s, 1)
+        return s
+
+    def vop(out, a, b, op, deps):
         for d in deps:
             wait(g.vector, "V", d)
-        for s in vsigs:
-            wait(g.vector, "V", s)
-        if b is None:
-            ins = g.vector.tensor_copy(out, a)
-        else:
-            ins = g.vector.tensor_tensor(out, a, b, op)
-        ins.then_inc(T.sem[sig], 1)
-        bump(sig, 1)
+        s = fresh()
+        g.vector.tensor_tensor(out, a, b, op).then_inc(T.sem[s], 1)
+        return s
 
-    MUL, ADD = AluOpType.mult, AluOpType.add
+    def acopy(out, a, deps):
+        for d in deps:
+            wait(g.scalar, "C", d)
+        s = fresh()
+        g.scalar.activation(out, a, ActivationFunctionType.Copy).then_inc(T.sem[s], 1)
+        return s
 
-    def send(src, dst_ap, dests, sem, deps):
+    def dag(ops, H):
+        at = {}
+        pending = list(ops)
+        mine = [o[0] for o in ops]
+        pos = 0
+        while pending:
+            ready = [o for o in pending if all((d in at) or (d not in mine) for d in o[5])]
+            best = min(ready, key=lambda o: max([at.get(d, -1) for d in o[5]] + [-1]))
+            H[best[0]] = vop(best[1], best[2], best[3], best[4], [H[d] for d in best[5]])
+            at[best[0]] = pos
+            pos += 1
+            pending.remove(best)
+
+    def send(srcs, dst_ap, dests, sem, deps):
         for d in deps:
             wait(g, "G", d)
         for d in dests:
             assert topo.may_write(core, d)
         m = engines(core, dests)
         ids = [DstId(rid=topo.addr(d)[0], pnc=topo.addr(d)[1]) for d in dests]
-        tr = RemoteDMATransfer(dst_ids=ids, dma_engine_mask=m, remote_sem=T.sem[sem], srcs=[src],
-                               dsts=[dst_ap for _ in dests], alu_op=0)
+        tr = RemoteDMATransfer(dst_ids=ids, dma_engine_mask=m, remote_sem=T.sem[sem], srcs=list(srcs),
+                               dsts=[dst_ap for _ in dests], alu_op=(1 if len(srcs) > 1 else 0))
         g.remote_dma_fused([tr], local_sem=T.sem.loc)
         bump("loc", len(_bits(m)))
 
@@ -127,6 +152,7 @@ def rank_program(g, core, T, topo):
     g0p, g1p = sl(T.Pg, 0), sl(T.Pg, 1)
     Y0, Y1 = sl(T.Y, 0), sl(T.Y, 1)
     first = (k == 0 and i == 0)
+    H = {s: s for s in ["ldg", "ldx", "arrA", "arrB", "arrAm", "arrBm", "arrBz"]}
 
     g.sync.dma_start(T.G[:], T.gate[:]).then_inc(T.sem.ldg, 16)
     bump("ldg", 16)
@@ -134,85 +160,89 @@ def rank_program(g, core, T, topo):
     bump("ldx", 16)
 
     d1 = hop1_dests(k, i)
-    vop(g1p, G1, deps=["ldg"])
-    if d1:
-        if not first:
-            vop(A(i), G0, g1p, MUL, sig="sAB")
-        vop(sl(T.Pt, 0), X0, g1p, MUL, deps=["ldx"])
-        vop(B(i), X1, sl(T.Pt, 0), ADD, sig="sAB")
-        piece = B(i) if first else sl(T.AB, 2 * i, 2)
-        send(piece, piece, d1, "arr1", ["sAB"])
-
-    if i <= 1 and not first:
-        vop(g0p, G0)
-    opA = {0: A(0), 1: A(1)}
-    opB = {0: B(0), 1: A(1)}
-    if k < last:
-        if i == 0:
-            vop(sl(T.Ph, 1), B(0))
-            opB[0] = sl(T.Ph, 1)
-            if k > 0:
-                vop(sl(T.Pt, 1), A(0))
-                opA[0] = sl(T.Pt, 1)
-        elif i == 1:
-            vop(sl(T.Pt, 1), A(1))
-            opA[1] = opB[1] = sl(T.Pt, 1)
-
-    top = n if k < last else i
-    PA, PB = {1: A(0)}, {1: B(0)}
-    if k > 0:
-        for j in range(1, top):
-            tot = (j == n - 1)
-            out = T.AT[:] if tot else sl(T.Pa, j - 1)
-            a, b = (opA[0], opA[1]) if j == 1 else (A(j), PA[j])
-            vop(out, a, b, MUL, sig=("sAT" if tot else "v"), deps=["arr1"])
-            PA[j + 1] = out
-        if k < last:
-            send(T.AT[:], T.Am[:], hop2_dests(k, core), "arrAm", ["sAT"])
-    h = sl(T.Ph, 0)
-    for j in range(1, top):
-        tot = (j == n - 1)
-        out = T.BT[:] if tot else sl(T.Pq, j - 1)
-        a, b = (opB[0], opB[1]) if j == 1 else (A(j), PB[j])
-        vop(h, a, b, MUL, deps=["arr1"])
-        vop(out, B(j), h, ADD, sig=("sBT" if tot else "v"))
-        PB[j + 1] = out
-    if k < last:
-        send(T.BT[:], (T.Bz[:] if k == 0 else T.Bm[:]), hop2_dests(k, core), ("arrBz" if k == 0 else "arrBm"), ["sBT"])
-
-    alpha, beta = g0p, X0
-    if i > 0:
-        if k > 0:
-            alpha = sl(T.Pl, 0)
-            if i == 1:
-                vop(alpha, PA[1], g0p, MUL, deps=["arr1"])
-            else:
-                vop(alpha, G0, PA[i], MUL)
-        if i == 1:
-            vop(h, PB[1], g0p, MUL, deps=["arr1"])
-        else:
-            vop(h, G0, PB[i], MUL)
-        beta = Y0 if k == 0 else T.Be[:]
-        vop(beta, X0, h, ADD, sig=("sY0" if k == 0 else "v"), deps=["ldx"])
-
-    pm, pq = sl(T.Pm, 0), sl(T.Pm, 1)
-    y0_src, y1_src, y0_dep, y1_dep = Y0, Y1, "sY0", "sY1"
-    if k == 0:
-        if i == 0:
-            y0_src, y0_dep, y1_src, y1_dep = X0, "ldx", B(0), "sAB"
-    elif k == 1:
-        vop(pm, T.Bz[:], alpha, MUL, deps=["arrBz"])
-        vop(Y0, beta, pm, ADD, sig="sY0", deps=["ldx"])
-    else:
-        a0 = sl(T.Pl, 1)
-        vop(a0, T.Am[:], alpha, MUL, deps=["arrAm"])
-        vop(pm, T.Bm[:], alpha, MUL, deps=["arrBm"])
-        vop(T.Be2[:], beta, pm, ADD, deps=["ldx"])
-        vop(pq, T.Bz[:], a0, MUL, deps=["arrBz"])
-        vop(Y0, T.Be2[:], pq, ADD, sig="sY0")
     if not first:
-        vop(pm, Y0, g1p, MUL)
-        vop(Y1, X1, pm, ADD, sig="sY1", deps=["ldx"])
+        H["g"] = acopy(T.Pg[:], T.G[:], ["ldg"])
+    if sends_a(k, i):
+        H["A"] = vop(sl(T.Ab, i), G0, G1, MUL, ["ldg"])
+        send([sl(T.Ab, i)], sl(T.Ab, i), d1, "arrA", [H["A"]])
+    if d1:
+        if first:
+            H["T"] = vop(T.Tb[:], X0, G1, MUL, ["ldx", "ldg"])
+        else:
+            H["T"] = vop(T.Tb[:], X0, g1p, MUL, ["ldx", H["g"]])
+        send([T.Tb[:], X1], sl(T.Bb, i), d1, "arrB", [H["T"], "ldx"])
+    if k < last:
+        H["B"] = vop(sl(T.Bb, i), T.Tb[:], X1, ADD, [H["T"], "ldx"])
+
+    if k < last:
+        d2 = hop2_dests(k, core)
+        own = [H["A"]] if "A" in H else []
+        S0, S1, S2 = sl(T.Ps, 0), sl(T.Ps, 1), sl(T.Pt, 0)
+        H["S2"] = acopy(S2, sl(T.Ab, 3), ["arrA"] + own)
+        H["S1"] = vop(S1, sl(T.Ab, 2), sl(T.Ab, 3), MUL, ["arrA"] + own)
+        H["S0"] = vop(S0, sl(T.Ab, 1), S1, MUL, [H["S1"]])
+        if k > 0:
+            H["AT"] = vop(T.AT[:], sl(T.Ab, 0), S0, MUL, [H["S0"]])
+            send([T.AT[:]], T.Am[:], d2, "arrAm", [H["AT"]])
+        H["U01"] = vop(sl(T.U, 0, 2), sl(T.Bb, 0, 2), T.Ps[:], MUL, ["arrB", H["B"], H["S0"], H["S1"]])
+        H["U2"] = vop(sl(T.U, 2), sl(T.Bb, 2), S2, MUL, ["arrB", H["B"], H["S2"]])
+        send([sl(T.U, 0), sl(T.U, 1), sl(T.U, 2), sl(T.Bb, 3)], (T.Bz[:] if k == 0 else T.Bm[:]), d2,
+             ("arrBz" if k == 0 else "arrBm"), [H["U01"], H["U2"], H["B"], "arrB"])
+
+    alpha, alpha1 = g0p, sl(T.Pa, 1)
+    beta, beta1 = X0, sl(T.Be, 1)
+    acc, tg = sl(T.Pc, 0), sl(T.Pc, 1)
+    ops = []
+    nb = "ldx"
+    na = "g"
+    if i > 0:
+        wt, wn = {i - 1: g0p}, {i - 1: "g"}
+        for j in range(i - 1, 0, -1):
+            wt[j - 1], wn[j - 1] = sl(T.Pw, j - 1), "w%d" % (j - 1)
+            ops.append((wn[j - 1], wt[j - 1], sl(T.Ab, j), wt[j], MUL, ["arrA", wn[j]]))
+        if k > 0:
+            alpha, na = sl(T.Pa, 0), "al"
+            ops.append(("al", alpha, sl(T.Ab, 0), wt[0], MUL, ["arrA", wn[0]]))
+        beta = Y0 if k == 0 else sl(T.Be, 0)
+        ops.append(("p%d" % (i - 1), acc, sl(T.Bb, i - 1), g0p, MUL, ["arrB", "g"]))
+        for j in range(i - 2, -1, -1):
+            ops.append(("p%d" % j, sl(T.Pr, j), sl(T.Bb, j), wt[j], MUL, ["arrB", wn[j]]))
+        prev = "p%d" % (i - 1)
+        ops.append(("q", (beta if i == 1 else acc), X0, acc, ADD, ["ldx", prev]))
+        prev = "q"
+        for j in range(i - 2, -1, -1):
+            ops.append(("q%d" % j, (beta if j == 0 else acc), sl(T.Pr, j), acc, ADD, ["p%d" % j, prev]))
+            prev = "q%d" % j
+        nb = prev
+    if k > 0:
+        ops.append(("al1", alpha1, G1, alpha, MUL, ["ldg", na]))
+    if not first:
+        ops.append(("tg", tg, beta, g1p, MUL, [nb, "g"]))
+        ops.append(("b1", (Y1 if k == 0 else beta1), X1, tg, ADD, ["ldx", "tg"]))
+    dag(ops, H)
+
+    if k == 0:
+        if first:
+            y0_src, y0_dep, y1_src, y1_dep = X0, "ldx", sl(T.Bb, 0), H["B"]
+        else:
+            y0_src, y0_dep, y1_src, y1_dep = Y0, H[nb], Y1, H["b1"]
+    else:
+        b0, b0n, b1, b1n, a0, a0n, a1, a1n = beta, nb, beta1, "b1", alpha, na, alpha1, "al1"
+        if k == last:
+            dag([("a0", sl(T.Pn, 0), T.Am[:], alpha, MUL, ["arrAm", na]),
+                 ("a1", sl(T.Pn, 1), T.Am[:], alpha1, MUL, ["arrAm", "al1"])], H)
+            dag([("m0", sl(T.Pm, 0), T.Bm[:], alpha, MUL, ["arrBm", na]),
+                 ("m1", sl(T.Pm, 1), T.Bm[:], alpha1, MUL, ["arrBm", "al1"]),
+                 ("e0", sl(T.Be2, 0), beta, sl(T.Pm, 0), ADD, [nb, "m0"]),
+                 ("e1", sl(T.Be2, 1), beta1, sl(T.Pm, 1), ADD, ["b1", "m1"])], H)
+            b0, b0n, b1, b1n = sl(T.Be2, 0), "e0", sl(T.Be2, 1), "e1"
+            a0, a0n, a1, a1n = sl(T.Pn, 0), "a0", sl(T.Pn, 1), "a1"
+        pr = T.Ps if k == last else T.Pm
+        dag([("z0", sl(pr, 0), T.Bz[:], a0, MUL, ["arrBz", a0n]),
+             ("z1", sl(pr, 1), T.Bz[:], a1, MUL, ["arrBz", a1n]),
+             ("y0", Y0, b0, sl(pr, 0), ADD, [b0n, "z0"]),
+             ("y1", Y1, b1, sl(pr, 1), ADD, [b1n, "z1"])], H)
+        y0_src, y0_dep, y1_src, y1_dep = Y0, H["y0"], Y1, H["y1"]
 
     wait(g.scalar, "C", y0_dep)
     g.scalar.dma_start(T.y[:, 0:W], y0_src).then_inc(T.sem.st, 16)

from concourse.bass import DstId, RemoteDMATransfer
from concourse.mybir import AluOpType, ActivationFunctionType

W = 256
BF = "bfloat16"
NC = 30
SCRATCH = {
    "G": ("sbuf", [128, 2 * W], BF),
    "X": ("sbuf", [128, 2 * W], BF),
    "Ab": ("sbuf", [128, 4 * W], BF),
    "Bb": ("sbuf", [128, 4 * W], BF),
    "Tb": ("sbuf", [128, W], BF),
    "U": ("sbuf", [128, 3 * W], BF),
    "AT": ("sbuf", [128, W], BF),
    "Am": ("sbuf", [128, W], BF),
    "Bm": ("sbuf", [128, W], BF),
    "Bz": ("sbuf", [128, W], BF),
    "Pr": ("sbuf", [128, 2 * W], BF),
    "Be": ("sbuf", [128, 2 * W], BF),
    "Be2": ("sbuf", [128, 2 * W], BF),
    "Y": ("sbuf", [128, 2 * W], BF),
    "Pg": ("psum", [128, 2 * W], "float32"),
    "Ps": ("psum", [128, 2 * W], "float32"),
    "Pt": ("psum", [128, 2 * W], "float32"),
    "Pw": ("psum", [128, 2 * W], "float32"),
    "Pa": ("psum", [128, 2 * W], "float32"),
    "Pc": ("psum", [128, 2 * W], "float32"),
    "Pm": ("psum", [128, 2 * W], "float32"),
    "Pn": ("psum", [128, 2 * W], "float32"),
}
SEMAPHORES = ["ldg", "ldx", "arrA", "arrB", "arrAm", "arrBm", "arrBz"] + ["c%d" % q for q in range(NC)] + ["loc", "st"]


def _bits(mask):
    return [b for b in range(32) if (mask >> b) & 1]


def rank_program(g, core, T, topo):
    if T.rank_of(core) is None:
        return
    groups = []
    for c in T.cores:
        if groups and topo.chip(groups[-1][0]) == topo.chip(c):
            groups[-1].append(c)
        else:
            groups.append([c])
    assert len(groups) == 3 and all(len(q) == 4 for q in groups)
    k = [core in q for q in groups].index(True)
    grp = groups[k]
    i = grp.index(core)
    n, last = 4, 2

    def sl(buf, j, m=1):
        return buf[:, j * W:(j + m) * W]

    def engines(src, dsts):
        m = topo.mask(src, dsts[0])
        for d in dsts[1:]:
            m &= topo.mask(src, d)
        return m

    def partner(a, b, c):
        sa = sorted(groups[a], key=lambda q: (topo.die(q), q))
        sb = sorted(groups[b], key=lambda q: (topo.die(q), q))
        return sb[sa.index(c)]

    def hop1_dests(kk, j):
        return [c for jj, c in enumerate(groups[kk]) if (jj != j if kk < last else jj > j)]

    def sends_a(kk, j):
        return bool(hop1_dests(kk, j)) and not (kk == 0 and j == 0)

    def hop2_dests(kk, c):
        return [partner(kk, b, c) for b in range(kk + 1, last + 1)]

    cnt = {}
    waited = {}

    def bump(name, m):
        cnt[name] = cnt.get(name, 0) + m

    def wait(q, qn, name):
        if cnt.get(name, 0) > waited.get((qn, name), 0):
            q.wait_ge(T.sem[name], cnt[name])
            waited[(qn, name)] = cnt[name]

    for j, c in enumerate(grp):
        if c != core and core in hop1_dests(k, j):
            e = len(_bits(engines(c, hop1_dests(k, j))))
            bump("arrB", e)
            if sends_a(k, j):
                bump("arrA", e)
    for kk in range(k):
        for c in groups[kk]:
            if core in hop2_dests(kk, c):
                e = len(_bits(engines(c, hop2_dests(kk, c))))
                if kk == 0:
                    bump("arrBz", e)
                else:
                    bump("arrAm", e)
                    bump("arrBm", e)

    MUL, ADD = AluOpType.mult, AluOpType.add
    used = [0]

    def fresh():
        s = "c%d" % used[0]
        used[0] += 1
        bump(s, 1)
        return s

    def vop(out, a, b, op, deps):
        for d in deps:
            wait(g.vector, "V", d)
        s = fresh()
        g.vector.tensor_tensor(out, a, b, op).then_inc(T.sem[s], 1)
        return s

    def acopy(out, a, deps):
        for d in deps:
            wait(g.scalar, "C", d)
        s = fresh()
        g.scalar.activation(out, a, ActivationFunctionType.Copy).then_inc(T.sem[s], 1)
        return s

    def dag(ops, H):
        at = {}
        pending = list(ops)
        mine = [o[0] for o in ops]
        pos = 0
        while pending:
            ready = [o for o in pending if all((d in at) or (d not in mine) for d in o[5])]
            best = min(ready, key=lambda o: max([at.get(d, -1) for d in o[5]] + [-1]))
            H[best[0]] = vop(best[1], best[2], best[3], best[4], [H[d] for d in best[5]])
            at[best[0]] = pos
            pos += 1
            pending.remove(best)

    def send(srcs, dst_ap, dests, sem, deps):
        for d in deps:
            wait(g, "G", d)
        for d in dests:
            assert topo.may_write(core, d)
        m = engines(core, dests)
        ids = [DstId(rid=topo.addr(d)[0], pnc=topo.addr(d)[1]) for d in dests]
        tr = RemoteDMATransfer(dst_ids=ids, dma_engine_mask=m, remote_sem=T.sem[sem], srcs=list(srcs),
                               dsts=[dst_ap for _ in dests], alu_op=(1 if len(srcs) > 1 else 0))
        g.remote_dma_fused([tr], local_sem=T.sem.loc)
        bump("loc", len(_bits(m)))

    G0, G1, X0, X1 = sl(T.G, 0), sl(T.G, 1), sl(T.X, 0), sl(T.X, 1)
    g0p, g1p = sl(T.Pg, 0), sl(T.Pg, 1)
    Y0, Y1 = sl(T.Y, 0), sl(T.Y, 1)
    first = (k == 0 and i == 0)
    H = {s: s for s in ["ldg", "ldx", "arrA", "arrB", "arrAm", "arrBm", "arrBz"]}

    g.sync.dma_start(T.G[:], T.gate[:]).then_inc(T.sem.ldg, 16)
    bump("ldg", 16)
    g.scalar.dma_start(T.X[:], T.x[:]).then_inc(T.sem.ldx, 16)
    bump("ldx", 16)

    d1 = hop1_dests(k, i)
    if not first:
        H["g"] = acopy(T.Pg[:], T.G[:], ["ldg"])
    if sends_a(k, i):
        H["A"] = vop(sl(T.Ab, i), G0, G1, MUL, ["ldg"])
        send([sl(T.Ab, i)], sl(T.Ab, i), d1, "arrA", [H["A"]])
    if d1:
        if first:
            H["T"] = vop(T.Tb[:], X0, G1, MUL, ["ldx", "ldg"])
        else:
            H["T"] = vop(T.Tb[:], X0, g1p, MUL, ["ldx", H["g"]])
        send([T.Tb[:], X1], sl(T.Bb, i), d1, "arrB", [H["T"], "ldx"])
    if k < last:
        H["B"] = vop(sl(T.Bb, i), T.Tb[:], X1, ADD, [H["T"], "ldx"])

    if k < last:
        d2 = hop2_dests(k, core)
        own = [H["A"]] if "A" in H else []
        S0, S1, S2 = sl(T.Ps, 0), sl(T.Ps, 1), sl(T.Pt, 0)
        H["S2"] = acopy(S2, sl(T.Ab, 3), ["arrA"] + own)
        H["S1"] = vop(S1, sl(T.Ab, 2), sl(T.Ab, 3), MUL, ["arrA"] + own)
        H["S0"] = vop(S0, sl(T.Ab, 1), S1, MUL, [H["S1"]])
        if k > 0:
            H["AT"] = vop(T.AT[:], sl(T.Ab, 0), S0, MUL, [H["S0"]])
            send([T.AT[:]], T.Am[:], d2, "arrAm", [H["AT"]])
        H["U01"] = vop(sl(T.U, 0, 2), sl(T.Bb, 0, 2), T.Ps[:], MUL, ["arrB", H["B"], H["S0"], H["S1"]])
        H["U2"] = vop(sl(T.U, 2), sl(T.Bb, 2), S2, MUL, ["arrB", H["B"], H["S2"]])
        send([sl(T.U, 0), sl(T.U, 1), sl(T.U, 2), sl(T.Bb, 3)], (T.Bz[:] if k == 0 else T.Bm[:]), d2,
             ("arrBz" if k == 0 else "arrBm"), [H["U01"], H["U2"], H["B"], "arrB"])

    alpha, alpha1 = g0p, sl(T.Pa, 1)
    beta, beta1 = X0, sl(T.Be, 1)
    acc, tg = sl(T.Pc, 0), sl(T.Pc, 1)
    ops = []
    nb = "ldx"
    na = "g"
    if i > 0:
        wt, wn = {i - 1: g0p}, {i - 1: "g"}
        for j in range(i - 1, 0, -1):
            wt[j - 1], wn[j - 1] = sl(T.Pw, j - 1), "w%d" % (j - 1)
            ops.append((wn[j - 1], wt[j - 1], sl(T.Ab, j), wt[j], MUL, ["arrA", wn[j]]))
        if k > 0:
            alpha, na = sl(T.Pa, 0), "al"
            ops.append(("al", alpha, sl(T.Ab, 0), wt[0], MUL, ["arrA", wn[0]]))
        beta = Y0 if k == 0 else sl(T.Be, 0)
        ops.append(("p%d" % (i - 1), acc, sl(T.Bb, i - 1), g0p, MUL, ["arrB", "g"]))
        for j in range(i - 2, -1, -1):
            ops.append(("p%d" % j, sl(T.Pr, j), sl(T.Bb, j), wt[j], MUL, ["arrB", wn[j]]))
        prev = "p%d" % (i - 1)
        ops.append(("q", (beta if i == 1 else acc), X0, acc, ADD, ["ldx", prev]))
        prev = "q"
        for j in range(i - 2, -1, -1):
            ops.append(("q%d" % j, (beta if j == 0 else acc), sl(T.Pr, j), acc, ADD, ["p%d" % j, prev]))
            prev = "q%d" % j
        nb = prev
    if k > 0:
        ops.append(("al1", alpha1, G1, alpha, MUL, ["ldg", na]))
    if not first:
        ops.append(("tg", tg, beta, g1p, MUL, [nb, "g"]))
        ops.append(("b1", (Y1 if k == 0 else beta1), X1, tg, ADD, ["ldx", "tg"]))
    dag(ops, H)

    if k == 0:
        if first:
            y0_src, y0_dep, y1_src, y1_dep = X0, "ldx", sl(T.Bb, 0), H["B"]
        else:
            y0_src, y0_dep, y1_src, y1_dep = Y0, H[nb], Y1, H["b1"]
    else:
        b0, b0n, b1, b1n, a0, a0n, a1, a1n = beta, nb, beta1, "b1", alpha, na, alpha1, "al1"
        if k == last:
            dag([("a0", sl(T.Pn, 0), T.Am[:], alpha, MUL, ["arrAm", na]),
                 ("a1", sl(T.Pn, 1), T.Am[:], alpha1, MUL, ["arrAm", "al1"])], H)
            dag([("m0", sl(T.Pm, 0), T.Bm[:], alpha, MUL, ["arrBm", na]),
                 ("m1", sl(T.Pm, 1), T.Bm[:], alpha1, MUL, ["arrBm", "al1"]),
                 ("e0", sl(T.Be2, 0), beta, sl(T.Pm, 0), ADD, [nb, "m0"]),
                 ("e1", sl(T.Be2, 1), beta1, sl(T.Pm, 1), ADD, ["b1", "m1"])], H)
            b0, b0n, b1, b1n = sl(T.Be2, 0), "e0", sl(T.Be2, 1), "e1"
            a0, a0n, a1, a1n = sl(T.Pn, 0), "a0", sl(T.Pn, 1), "a1"
        pr = T.Ps if k == last else T.Pm
        dag([("z0", sl(pr, 0), T.Bz[:], a0, MUL, ["arrBz", a0n]),
             ("z1", sl(pr, 1), T.Bz[:], a1, MUL, ["arrBz", a1n]),
             ("y0", Y0, b0, sl(pr, 0), ADD, [b0n, "z0"]),
             ("y1", Y1, b1, sl(pr, 1), ADD, [b1n, "z1"])], H)
        y0_src, y0_dep, y1_src, y1_dep = Y0, H["y0"], Y1, H["y1"]

    wait(g.scalar, "C", y0_dep)
    g.scalar.dma_start(T.y[:, 0:W], y0_src).then_inc(T.sem.st, 16)
    wait(g.sync, "S", y1_dep)
    g.sync.dma_start(T.y[:, W:2 * W], y1_src).then_inc(T.sem.st, 16)
    bump("st", 32)

    for name in SEMAPHORES:
        wait(g, "G", name)
